import numpy as np
import ml_dtypes


def mxq(x, axis, fmt="e4m3"):
    dtype, down = {"e4m3": (ml_dtypes.float8_e4m3fn, 7), "e5m2": (ml_dtypes.float8_e5m2, 14)}[fmt]
    v = np.moveaxis(np.asarray(x, np.float32).astype(ml_dtypes.bfloat16).astype(np.float64), axis, -1)
    blocks = v.reshape(v.shape[:-1] + (-1, 32))
    amax = np.abs(blocks).max(-1, keepdims=True)
    byte = np.maximum(np.where(amax > 0, np.frexp(amax)[1] - 1 + 127, 0) - down, 1)
    scale = np.exp2(byte - 127.0)
    codes = (blocks / scale).astype(np.float32).astype(dtype).astype(np.float64)
    return np.moveaxis((codes * scale).reshape(v.shape), -1, axis)


WIDE = False


def mx_kscale(k):
    if not WIDE:
        return np.ones(k)
    levels = np.array([10, -10, 5, -5, 0])
    if k % 512:
        return np.exp2(np.random.permutation(np.resize(levels, k // 32))).repeat(32)
    a = np.empty((k // 512, 16))
    for p in range(k // 512):
        a[p, :8] = np.random.permutation(np.resize(levels, 8))
        for g in range(8):
            far = levels[np.abs(levels - a[p, g]) >= 10]
            a[p, g + 8] = far[np.random.randint(len(far))]
    return np.exp2(a.ravel()).repeat(32)


def f64(x):
    return np.asarray(x).astype(np.float64)


def striped(idx):
    return np.tile(idx.reshape(-1, 16).T, (8, 1)).astype(np.uint16)


def unstriped(offs):
    return offs[:16].T.reshape(-1).astype(np.int64)


def striped8(idx):
    return np.concatenate([x.reshape(-1, 16).T for x in idx]).astype(np.uint16)


def runs(offs, k):
    lists = np.stack([offs[16 * r : 16 * r + 16].T.reshape(-1) for r in range(8)]).astype(np.int64)
    return lists[np.arange(k) % 512 // 64]


def pack_weight(w):
    k, n = w.shape
    w = f64(np.asarray(w, np.float32).astype(ml_dtypes.bfloat16)).reshape(k // 32, 32, n)
    amax = np.abs(w).max(1)
    byte = np.clip(np.where(amax > 0, np.frexp(amax)[1] - 1 + 127 - 7, 1), 1, 254)
    scaled = (w * np.exp2(127.0 - byte)[:, None, :]).reshape(k, n).astype(np.float32)
    words = np.ascontiguousarray(scaled.reshape(k // 512, 128, 4, n).transpose(0, 1, 3, 2)).astype(ml_dtypes.float8_e4m3fn).view(np.uint8)
    return words, np.ascontiguousarray(byte.astype(np.uint8).reshape(k // 512, 16, n))


def unpack_weight(words, scales):
    g, p, n, _ = words.shape
    vals = np.ascontiguousarray(words).view(ml_dtypes.float8_e4m3fn).astype(np.float64) * np.repeat(np.exp2(scales.astype(np.float64) - 127.0), 8, axis=1)[..., None]
    return vals.transpose(0, 1, 3, 2).reshape(g * 512, n)


def relu(v):
    return np.maximum(v, 0.0)

def planes(y):
    n, m = y.shape
    v = y.astype(np.float32).astype(ml_dtypes.bfloat16).astype(np.float64).reshape(n // 32, 32, m)
    top = np.abs(v).max(1)
    byte = np.clip(np.where(top > 0, np.frexp(top)[1] - 1 + 127 - 7, 1), 1, 254)
    codes = (v * np.exp2(127.0 - byte)[:, None, :]).reshape(n, m).astype(np.float32).astype(ml_dtypes.float8_e4m3fn).view(np.uint8)
    words = codes.reshape(n // 512, 128, 4, m).transpose(0, 1, 3, 2)
    return np.ascontiguousarray(words), np.ascontiguousarray(byte.astype(np.uint8).reshape(n // 512, 16, m))


K, T, S, N, H, U = 512, 2048, 512, 512, 512, 1024


def setup_inputs():
    n = np.random.standard_normal
    s = mx_kscale(K)[:, None]
    u = mx_kscale(H)
    packed_xT = pack_weight(n((K, T)) * s)
    packed_w3 = pack_weight(n((H, N)) / np.sqrt(H) / u[:, None])
    perm = np.stack([np.random.permutation(U) for _ in range(8)])
    return {
        "x_words": packed_xT[0],
        "x_scales": packed_xT[1],
        "w1": (n((K, H)) / np.sqrt(K) / s * u).astype(np.float32),
        "w2": (n((K, H)) / np.sqrt(K) / s * u).astype(np.float32),
        "w3_words": packed_w3[0],
        "w3_scales": packed_w3[1],
        "offs": striped(np.random.permutation(T)[:S]),
        "img": striped(np.random.permutation(T)[:S]),
        "la": striped8(perm[:, :S]),
        "lb": striped8(perm[:, S:]),
    }


def reference(x_words, x_scales, w1, w2, w3_words, w3_scales, offs, img, la, lb):
    x_img = unpack_weight(x_words, x_scales)[:, unstriped(img)]
    e = mxq(f64(w2), 0, "e4m3").T @ x_img
    eb = relu(e)
    xq = unpack_weight(x_words, x_scales)[:, unstriped(offs)]
    y = mxq(f64(w1), 0, "e4m3").T @ xq
    p = np.zeros((H, U))
    p[np.arange(H)[:, None], runs(la, H)] = y
    z = p.copy()
    z[np.arange(H)[:, None], runs(lb, H)] = eb
    out_0 = unpack_weight(w3_words, w3_scales).T @ mxq(z, 0, "e4m3")
    return (out_0,) + planes(out_0)

@@ -1,0 +1,194 @@
+from contextlib import ExitStack
+
+import concourse.mybir as mybir
+
+K, T, S, N, H, U = 512, 2048, 512, 512, 512, 1024
+FLOPS = 2 * K * H * S * 2 + 2 * H * N * U
+
+F32 = mybir.dt.float32
+BF16 = mybir.dt.bfloat16
+I32 = mybir.dt.int32
+U32 = mybir.dt.uint32
+U16 = mybir.dt.uint16
+U8 = mybir.dt.uint8
+FP8X4 = mybir.dt.float8_e4m3fn_x4
+RELU = mybir.ActivationFunctionType.Relu
+
+P = 128
+PACK = 4
+CHUNKS = (128, 256, 256, 256, 128)
+SCALAR_CHUNKS = (2, 3)
+VECTOR_BANK = (1, 2)
+ORDER = (2, 0, 1, 3)
+CAST_SPLIT = 84
+
+
+def load_scale_rows(nc, plane, rows):
+    width = rows.shape[1] // 4
+    for q in range(4):
+        src = rows[4 * q : 4 * q + 4, :].bitcast(I32).unsqueeze(0).to_broadcast([8, 4, width])
+        nc.sync.dma_start(out=plane[32 * q : 32 * q + 32, :].bitcast(I32), in_=src)
+
+
+def cast_weights(engine_copy, grouped, raw, m0, m1):
+    engine_copy(
+        out=grouped[:].rearrange("p (t m j) -> p m j t", t=PACK, j=PACK)[:, m0:m1],
+        in_=raw[:].rearrange("p j (m t) -> p m j t", t=PACK)[:, m0:m1],
+    )
+
+
+def quantize(nc, codes, scales, values):
+    nc.vector.quantize_mx(out=codes.bitcast(FP8X4), scales=scales, in_=values)
+
+
+def one_pass(nc, out, w_codes, w_scales, t, codes, scales):
+    cols = slice(P * t, P * (t + 1))
+    nc.tensor.matmul_mx(out=out, lhsT=w_codes[:, cols].bitcast(FP8X4), lhsT_scale=w_scales[:, cols],
+                        rhs=codes.bitcast(FP8X4), rhs_scale=scales, start=True, stop=True)
+
+
+def tile_picked_interl_relu_po_kernel(
+    tc, x_words, x_scales, w1, w2, w3_words, w3_scales, offs, img, la, lb, out_0, out_1, out_2
+):
+    nc = tc.nc
+    with ExitStack() as ctx:
+        lists = ctx.enter_context(tc.tile_pool(name="lists", bufs=1))
+        keep = ctx.enter_context(tc.tile_pool(name="keep", bufs=1))
+        proj = ctx.enter_context(tc.psum_pool(name="proj", bufs=3))
+        last = ctx.enter_context(tc.psum_pool(name="last", bufs=5))
+
+        offs_sb = lists.tile([P, S // 16], U16, name="offs_sb")
+        img_sb = lists.tile([P, S // 16], U16, name="img_sb")
+        la_sb = lists.tile([P, S // 16], U16, name="la_sb")
+        lb_sb = lists.tile([P, S // 16], U16, name="lb_sb")
+        x_plane = keep.tile([P, T], U8, name="x_plane", align_bytes=64)
+        x_table = keep.tile([P, T], I32, name="x_table", align_bytes=64)
+        w1_raw = keep.tile([P, PACK, H], F32, name="w1_raw", align_bytes=64)
+        w2_raw = keep.tile([P, PACK, H], F32, name="w2_raw", tag="late", align_bytes=64)
+        w3_table = keep.tile([P, N], I32, name="w3_table", align_bytes=64)
+        w3_plane = keep.tile([P, N], U8, name="w3_plane", align_bytes=64)
+
+        nc.sync.dma_start(offs_sb[:], offs)
+        nc.sync.dma_start(img_sb[:], img)
+        load_scale_rows(nc, x_plane, x_scales[0])
+        nc.sync.dma_start(out=x_table[:], in_=x_words[0].rearrange("p n t -> p (n t)").bitcast(I32))
+        nc.sync.dma_start(out=w1_raw[:], in_=w1.rearrange("(p j) c -> p j c", j=PACK))
+        nc.sync.dma_start(out=w3_table[:], in_=w3_words[0].rearrange("p n t -> p (n t)").bitcast(I32))
+        load_scale_rows(nc, w3_plane, w3_scales[0])
+        nc.sync.dma_start(la_sb[:], la)
+        nc.sync.dma_start(lb_sb[:], lb)
+        nc.sync.dma_start(out=w2_raw[:], in_=w2.rearrange("(p j) c -> p j c", j=PACK))
+
+        txt_scales = keep.tile([P, S], U8, name="txt_scales", align_bytes=64)
+        img_scales = keep.tile([P, S], U8, name="img_scales", align_bytes=64)
+        txt_codes = keep.tile([P, S], I32, name="txt_codes", align_bytes=64)
+        img_codes = keep.tile([P, S], I32, name="img_codes", align_bytes=64)
+        nc.vector.tensor_copy(txt_scales[:], x_plane[:].indirect(offs_sb[:]))
+        nc.vector.tensor_copy(img_scales[:], x_plane[:].indirect(img_sb[:]))
+        nc.vector.tensor_copy(txt_codes[:].bitcast(U32), x_table[:].bitcast(U32).indirect(offs_sb[:]))
+        nc.vector.tensor_copy(img_codes[:].bitcast(U32), x_table[:].bitcast(U32).indirect(img_sb[:]))
+
+        w1_bf = keep.tile([P, PACK * H], BF16, name="w1_bf", align_bytes=64)
+        w1_codes = keep.tile([P, H], I32, name="w1_codes", align_bytes=64)
+        w1_plane = keep.tile([P, H], U8, name="w1_plane", align_bytes=64)
+        cast_weights(nc.vector.tensor_copy, w1_bf, w1_raw, 0, CAST_SPLIT)
+        cast_weights(nc.scalar.copy, w1_bf, w1_raw, CAST_SPLIT, P)
+        for c0, c1 in ((256, 384), (0, 256), (384, 512)):
+            quantize(nc, w1_codes[:, c0:c1], w1_plane[:, c0:c1], w1_bf[:, PACK * c0 : PACK * c1])
+
+        w3_codes = keep.tile([P, N], I32, name="w3_codes", align_bytes=64)
+        w3_dealt = keep.tile([P, N], U8, name="w3_dealt", align_bytes=64)
+        nc.vector.tensor_copy(out=w3_codes[:].rearrange("p (t m) -> p m t", t=PACK),
+                              in_=w3_table[:].rearrange("p (m t) -> p m t", t=PACK))
+        nc.vector.tensor_copy(out=w3_dealt[:].rearrange("p (t m) -> p m t", t=PACK),
+                              in_=w3_plane[:].rearrange("p (m t) -> p m t", t=PACK))
+
+        z = [keep.tile([P, U], F32, name="z%d" % t, align_bytes=64) for t in range(PACK)]
+
+        def project_text(t, j0, j1, tag):
+            bank = proj.tile([P, j1 - j0], F32, name="bank", tag="bank")
+            one_pass(nc, bank[:], w1_codes, w1_plane, t, txt_codes[:, j0:j1], txt_scales[:, j0:j1])
+            y = keep.tile([P, j1 - j0], F32, name="y", tag=tag, align_bytes=64)
+            nc.scalar.copy(out=y[:], in_=bank[:])
+            nc.vector.tensor_copy(z[t][:].indirect(la_sb[:, j0 // 16 : j1 // 16]), y[:])
+
+        def project_image(t, tag):
+            bank = proj.tile([P, S], F32, name="bank", tag="bank")
+            one_pass(nc, bank[:], w2_codes, w2_plane, t, img_codes[:], img_scales[:])
+            eb = keep.tile([P, S], F32, name="eb", tag=tag, align_bytes=64)
+            nc.scalar.activation(out=eb[:], in_=bank[:], func=RELU)
+            nc.vector.tensor_copy(z[t][:].indirect(lb_sb[:]), eb[:])
+
+        project_text(ORDER[0], 0, S // 2, "y0a")
+        project_text(ORDER[0], S // 2, S, "y0b")
+        project_text(ORDER[1], 0, S, "y1")
+
+        w2_bf = keep.tile([P, PACK * H], BF16, name="w2_bf", align_bytes=64)
+        w2_codes = keep.tile([P, H], I32, name="w2_codes", align_bytes=64)
+        w2_plane = keep.tile([P, H], U8, name="w2_plane", align_bytes=64)
+        cast_weights(nc.scalar.copy, w2_bf, w2_raw, 0, P)
+        quantize(nc, w2_codes[:], w2_plane[:], w2_bf[:])
+
+        starts = [sum(CHUNKS[:c]) for c in range(len(CHUNKS))]
+        z_bf = [keep.tile([P, n, PACK], BF16, name="z_bf%d" % c, align_bytes=64) for c, n in enumerate(CHUNKS)]
+
+        def regroup(copy, t, c):
+            copy(out=z_bf[c][:, :, t], in_=z[t][:, starts[c] : starts[c] + CHUNKS[c]])
+
+        project_text(ORDER[2], 0, S, "late")
+        for t in ORDER[:3]:
+            project_image(t, "eb%d" % t)
+        project_text(ORDER[3], 0, S, "y3")
+        for c in range(len(CHUNKS)):
+            regroup(nc.scalar.copy, ORDER[0], c)
+        project_image(ORDER[3], "z%d" % ORDER[0])
+        for t in ORDER[1:3]:
+            for c in range(len(CHUNKS)):
+                regroup(nc.scalar.copy, t, c)
+        for c in SCALAR_CHUNKS:
+            regroup(nc.scalar.copy, ORDER[3], c)
+
+        out_rows = out_0.rearrange("(p t) w -> p t w", t=PACK)
+        out_words = out_1[0].rearrange("p n t -> p (n t)").bitcast(I32)
+        out_plane = keep.tile([P, U], U8, name="out_plane", align_bytes=64)
+
+        def quantize_z(c):
+            n = CHUNKS[c]
+            z_codes = keep.tile([P, n], I32, name="z_codes%d" % c, align_bytes=64)
+            z_plane = keep.tile([P, n], U8, name="z_plane%d" % c, align_bytes=64)
+            quantize(nc, z_codes[:], z_plane[:], z_bf[c][:].rearrange("p n t -> p (n t)"))
+            return z_codes, z_plane
+
+        def multiply(c, z_codes, z_plane):
+            n = CHUNKS[c]
+            cols = slice(starts[c], starts[c] + n)
+            result = keep.tile([P, PACK, n], F32, name="result%d" % c, align_bytes=64)
+            rounded = keep.tile([P, n, PACK], BF16, name="rounded%d" % c, align_bytes=64)
+            per_bank = 512 // n
+            for t0 in range(0, PACK, per_bank):
+                acc = last.tile([P, per_bank, n], F32, name="acc", tag="acc")
+                for i in range(per_bank):
+                    one_pass(nc, acc[:, i, :], w3_codes, w3_dealt, t0 + i, z_codes[:], z_plane[:])
+                if c == len(CHUNKS) - 1:
+                    nc.scalar.copy(out=rounded[:], in_=acc[:].rearrange("p t n -> p n t"))
+                copy = nc.vector.tensor_copy if (c, t0) == VECTOR_BANK else nc.scalar.copy
+                copy(out=result[:, t0 : t0 + per_bank, :], in_=acc[:])
+                nc.sync.dma_start(out=out_rows[:, t0 : t0 + per_bank, cols], in_=result[:, t0 : t0 + per_bank, :])
+            if c < len(CHUNKS) - 1:
+                nc.vector.tensor_copy(out=rounded[:].rearrange("p (c i) t -> p c t i", i=4),
+                                      in_=result[:].rearrange("p t (c i) -> p c t i", i=4))
+            codes = keep.tile([P, n], I32, name="out_codes%d" % c, align_bytes=64)
+            quantize(nc, codes[:], out_plane[:, cols], rounded[:].rearrange("p n t -> p (n t)"))
+            nc.sync.dma_start(out=out_words[:, cols], in_=codes[:])
+
+        regroup(nc.vector.tensor_copy, ORDER[3], 0)
+        regroup(nc.vector.tensor_copy, ORDER[3], 1)
+        z_quantised = [quantize_z(c) for c in range(3)]
+        regroup(nc.vector.tensor_copy, ORDER[3], 4)
+        z_quantised.extend(quantize_z(c) for c in range(3, 5))
+        for c in range(len(CHUNKS)):
+            multiply(c, *z_quantised[c])
+        for q in range(4):
+            queue = nc.scalar if q % 2 else nc.sync
+            queue.dma_start(out=out_2[0, 4 * q : 4 * q + 4, :].bitcast(I32),
+                            in_=out_plane[32 * q : 32 * q + 4, :].bitcast(I32))

@@ -19,8 +19,9 @@ PACK = 4
 CHUNKS = (128, 256, 256, 256, 128)
 SCALAR_CHUNKS = (2, 3)
 VECTOR_BANK = (1, 2)
+BANK_STORES = (1,)
+WORD_STORES = {2: 0, 4: 640}
 ORDER = (2, 0, 1, 3)
-CAST_SPLIT = 84
 
 
 def load_scale_rows(nc, plane, rows):
@@ -30,10 +31,10 @@ def load_scale_rows(nc, plane, rows):
         nc.sync.dma_start(out=plane[32 * q : 32 * q + 32, :].bitcast(I32), in_=src)
 
 
-def cast_weights(engine_copy, grouped, raw, m0, m1):
-    engine_copy(
-        out=grouped[:].rearrange("p (t m j) -> p m j t", t=PACK, j=PACK)[:, m0:m1],
-        in_=raw[:].rearrange("p j (m t) -> p m j t", t=PACK)[:, m0:m1],
+def cast_weights(copy, grouped, raw, t0, t1):
+    copy(
+        out=grouped[:].rearrange("p (t m j) -> p m t j", t=PACK, j=PACK)[:, :, t0:t1],
+        in_=raw[:].rearrange("p j (m t) -> p m t j", t=PACK)[:, :, t0:t1],
     )
 
 
@@ -91,17 +92,20 @@ def tile_picked_interl_relu_po_kernel(
         w1_bf = keep.tile([P, PACK * H], BF16, name="w1_bf", align_bytes=64)
         w1_codes = keep.tile([P, H], I32, name="w1_codes", align_bytes=64)
         w1_plane = keep.tile([P, H], U8, name="w1_plane", align_bytes=64)
-        cast_weights(nc.vector.tensor_copy, w1_bf, w1_raw, 0, CAST_SPLIT)
-        cast_weights(nc.scalar.copy, w1_bf, w1_raw, CAST_SPLIT, P)
-        for c0, c1 in ((256, 384), (0, 256), (384, 512)):
+
+        def quantize_w1(copy, t0, t1):
+            cast_weights(copy, w1_bf, w1_raw, t0, t1)
+            c0, c1 = P * t0, P * t1
             quantize(nc, w1_codes[:, c0:c1], w1_plane[:, c0:c1], w1_bf[:, PACK * c0 : PACK * c1])
+
+        quantize_w1(nc.vector.tensor_copy, 2, 3)
 
         w3_codes = keep.tile([P, N], I32, name="w3_codes", align_bytes=64)
         w3_dealt = keep.tile([P, N], U8, name="w3_dealt", align_bytes=64)
         nc.vector.tensor_copy(out=w3_codes[:].rearrange("p (t m) -> p m t", t=PACK),
                               in_=w3_table[:].rearrange("p (m t) -> p m t", t=PACK))
-        nc.vector.tensor_copy(out=w3_dealt[:].rearrange("p (t m) -> p m t", t=PACK),
-                              in_=w3_plane[:].rearrange("p (m t) -> p m t", t=PACK))
+        nc.vector.tensor_copy(out=w3_dealt[:].rearrange("p (t m) -> p t m", t=PACK),
+                              in_=w3_plane[:].rearrange("p (m t) -> p t m", t=PACK))
 
         z = [keep.tile([P, U], F32, name="z%d" % t, align_bytes=64) for t in range(PACK)]
 
@@ -121,12 +125,14 @@ def tile_picked_interl_relu_po_kernel(
 
         project_text(ORDER[0], 0, S // 2, "y0a")
         project_text(ORDER[0], S // 2, S, "y0b")
+        quantize_w1(nc.scalar.copy, 0, 2)
+        quantize_w1(nc.scalar.copy, 3, 4)
         project_text(ORDER[1], 0, S, "y1")
 
         w2_bf = keep.tile([P, PACK * H], BF16, name="w2_bf", align_bytes=64)
         w2_codes = keep.tile([P, H], I32, name="w2_codes", align_bytes=64)
         w2_plane = keep.tile([P, H], U8, name="w2_plane", align_bytes=64)
-        cast_weights(nc.scalar.copy, w2_bf, w2_raw, 0, P)
+        cast_weights(nc.scalar.copy, w2_bf, w2_raw, 0, PACK)
         quantize(nc, w2_codes[:], w2_plane[:], w2_bf[:])
 
         starts = [sum(CHUNKS[:c]) for c in range(len(CHUNKS))]
@@ -141,15 +147,21 @@ def tile_picked_interl_relu_po_kernel(
         project_text(ORDER[3], 0, S, "y3")
         for c in range(len(CHUNKS)):
             regroup(nc.scalar.copy, ORDER[0], c)
-        project_image(ORDER[3], "z%d" % ORDER[0])
-        for t in ORDER[1:3]:
+        bank = proj.tile([P, S], F32, name="bank", tag="bank")
+        one_pass(nc, bank[:], w2_codes, w2_plane, ORDER[3], img_codes[:], img_scales[:])
+        for half, t in enumerate(ORDER[1:3]):
             for c in range(len(CHUNKS)):
                 regroup(nc.scalar.copy, t, c)
+            j0, j1 = half * S // 2, (half + 1) * S // 2
+            eb = keep.tile([P, S // 2], F32, name="eb", tag="z%d" % (ORDER[0] if half == 0 else t), align_bytes=64)
+            nc.scalar.activation(out=eb[:], in_=bank[:, j0:j1], func=RELU)
+            nc.vector.tensor_copy(z[ORDER[3]][:].indirect(lb_sb[:, j0 // 16 : j1 // 16]), eb[:])
         for c in SCALAR_CHUNKS:
             regroup(nc.scalar.copy, ORDER[3], c)
 
         out_rows = out_0.rearrange("(p t) w -> p t w", t=PACK)
         out_words = out_1[0].rearrange("p n t -> p (n t)").bitcast(I32)
+        out_codes = keep.tile([P, U], I32, name="out_codes", align_bytes=64)
         out_plane = keep.tile([P, U], U8, name="out_plane", align_bytes=64)
 
         def quantize_z(c):
@@ -166,20 +178,27 @@ def tile_picked_interl_relu_po_kernel(
             rounded = keep.tile([P, n, PACK], BF16, name="rounded%d" % c, align_bytes=64)
             per_bank = 512 // n
             for t0 in range(0, PACK, per_bank):
-                acc = last.tile([P, per_bank, n], F32, name="acc", tag="acc")
+                if c < 2:
+                    acc = proj.tile([P, per_bank, n], F32, name="acc", tag="bank")
+                else:
+                    acc = last.tile([P, per_bank, n], F32, name="acc", tag="acc")
                 for i in range(per_bank):
                     one_pass(nc, acc[:, i, :], w3_codes, w3_dealt, t0 + i, z_codes[:], z_plane[:])
                 if c == len(CHUNKS) - 1:
                     nc.scalar.copy(out=rounded[:], in_=acc[:].rearrange("p t n -> p n t"))
                 copy = nc.vector.tensor_copy if (c, t0) == VECTOR_BANK else nc.scalar.copy
                 copy(out=result[:, t0 : t0 + per_bank, :], in_=acc[:])
-                nc.sync.dma_start(out=out_rows[:, t0 : t0 + per_bank, cols], in_=result[:, t0 : t0 + per_bank, :])
+                if c in BANK_STORES:
+                    nc.sync.dma_start(out=out_rows[:, t0 : t0 + per_bank, cols], in_=result[:, t0 : t0 + per_bank, :])
+            if c not in BANK_STORES:
+                nc.sync.dma_start(out=out_rows[:, :, cols], in_=result[:])
             if c < len(CHUNKS) - 1:
                 nc.vector.tensor_copy(out=rounded[:].rearrange("p (c i) t -> p c t i", i=4),
                                       in_=result[:].rearrange("p t (c i) -> p c t i", i=4))
-            codes = keep.tile([P, n], I32, name="out_codes%d" % c, align_bytes=64)
-            quantize(nc, codes[:], out_plane[:, cols], rounded[:].rearrange("p n t -> p (n t)"))
-            nc.sync.dma_start(out=out_words[:, cols], in_=codes[:])
+            quantize(nc, out_codes[:, cols], out_plane[:, cols], rounded[:].rearrange("p n t -> p (n t)"))
+            if c in WORD_STORES:
+                done = slice(WORD_STORES[c], starts[c] + n)
+                nc.sync.dma_start(out=out_words[:, done], in_=out_codes[:, done])
 
         regroup(nc.vector.tensor_copy, ORDER[3], 0)
         regroup(nc.vector.tensor_copy, ORDER[3], 1)

@@ -17,10 +17,9 @@ RELU = mybir.ActivationFunctionType.Relu
 P = 128
 PACK = 4
 CHUNKS = (128, 256, 256, 256, 128)
-SCALAR_CHUNKS = (2, 3)
 VECTOR_BANK = (1, 2)
 BANK_STORES = (1,)
-WORD_STORES = {2: 0, 4: 640}
+WORD_STORES = {2: 0, 3: 640, 4: 896}
 ORDER = (2, 0, 1, 3)
 
 
@@ -31,10 +30,10 @@ def load_scale_rows(nc, plane, rows):
         nc.sync.dma_start(out=plane[32 * q : 32 * q + 32, :].bitcast(I32), in_=src)
 
 
-def cast_weights(copy, grouped, raw, t0, t1):
+def cast_weights(copy, grouped, raw, slots):
     copy(
-        out=grouped[:].rearrange("p (t m j) -> p m t j", t=PACK, j=PACK)[:, :, t0:t1],
-        in_=raw[:].rearrange("p j (m t) -> p m t j", t=PACK)[:, :, t0:t1],
+        out=grouped[:].rearrange("p (t m j) -> p m t j", m=P, j=PACK),
+        in_=raw[:].rearrange("p j (m t) -> p m t j", t=PACK)[:, :, slots],
     )
 
 
@@ -69,9 +68,9 @@ def tile_picked_interl_relu_po_kernel(
         w3_table = keep.tile([P, N], I32, name="w3_table", align_bytes=64)
         w3_plane = keep.tile([P, N], U8, name="w3_plane", align_bytes=64)
 
+        load_scale_rows(nc, x_plane, x_scales[0])
         nc.sync.dma_start(offs_sb[:], offs)
         nc.sync.dma_start(img_sb[:], img)
-        load_scale_rows(nc, x_plane, x_scales[0])
         nc.sync.dma_start(out=x_table[:], in_=x_words[0].rearrange("p n t -> p (n t)").bitcast(I32))
         nc.sync.dma_start(out=w1_raw[:], in_=w1.rearrange("(p j) c -> p j c", j=PACK))
         nc.sync.dma_start(out=w3_table[:], in_=w3_words[0].rearrange("p n t -> p (n t)").bitcast(I32))
@@ -89,16 +88,16 @@ def tile_picked_interl_relu_po_kernel(
         nc.vector.tensor_copy(txt_codes[:].bitcast(U32), x_table[:].bitcast(U32).indirect(offs_sb[:]))
         nc.vector.tensor_copy(img_codes[:].bitcast(U32), x_table[:].bitcast(U32).indirect(img_sb[:]))
 
-        w1_bf = keep.tile([P, PACK * H], BF16, name="w1_bf", align_bytes=64)
-        w1_codes = keep.tile([P, H], I32, name="w1_codes", align_bytes=64)
-        w1_plane = keep.tile([P, H], U8, name="w1_plane", align_bytes=64)
+        def quantize_weights(copy, raw, slots, tag):
+            count = len(range(PACK)[slots])
+            grouped = keep.tile([P, count * H], BF16, name="grouped", tag=tag, align_bytes=64)
+            codes = keep.tile([P, count * P], I32, name="codes", tag=tag + "_codes", align_bytes=64)
+            plane = keep.tile([P, count * P], U8, name="plane", tag=tag + "_plane", align_bytes=64)
+            cast_weights(copy, grouped, raw, slots)
+            quantize(nc, codes[:], plane[:], grouped[:])
+            return {t: (codes, plane, i) for i, t in enumerate(range(PACK)[slots])}
 
-        def quantize_w1(copy, t0, t1):
-            cast_weights(copy, w1_bf, w1_raw, t0, t1)
-            c0, c1 = P * t0, P * t1
-            quantize(nc, w1_codes[:, c0:c1], w1_plane[:, c0:c1], w1_bf[:, PACK * c0 : PACK * c1])
-
-        quantize_w1(nc.vector.tensor_copy, 2, 3)
+        w1_mx = quantize_weights(nc.vector.tensor_copy, w1_raw, slice(2, 3), "w1_first")
 
         w3_codes = keep.tile([P, N], I32, name="w3_codes", align_bytes=64)
         w3_dealt = keep.tile([P, N], U8, name="w3_dealt", align_bytes=64)
@@ -111,35 +110,30 @@ def tile_picked_interl_relu_po_kernel(
 
         def project_text(t, j0, j1, tag):
             bank = proj.tile([P, j1 - j0], F32, name="bank", tag="bank")
-            one_pass(nc, bank[:], w1_codes, w1_plane, t, txt_codes[:, j0:j1], txt_scales[:, j0:j1])
+            one_pass(nc, bank[:], *w1_mx[t], txt_codes[:, j0:j1], txt_scales[:, j0:j1])
             y = keep.tile([P, j1 - j0], F32, name="y", tag=tag, align_bytes=64)
             nc.scalar.copy(out=y[:], in_=bank[:])
             nc.vector.tensor_copy(z[t][:].indirect(la_sb[:, j0 // 16 : j1 // 16]), y[:])
 
         def project_image(t, tag):
             bank = proj.tile([P, S], F32, name="bank", tag="bank")
-            one_pass(nc, bank[:], w2_codes, w2_plane, t, img_codes[:], img_scales[:])
+            one_pass(nc, bank[:], *w2_mx[t], img_codes[:], img_scales[:])
             eb = keep.tile([P, S], F32, name="eb", tag=tag, align_bytes=64)
             nc.scalar.activation(out=eb[:], in_=bank[:], func=RELU)
             nc.vector.tensor_copy(z[t][:].indirect(lb_sb[:]), eb[:])
 
         project_text(ORDER[0], 0, S // 2, "y0a")
         project_text(ORDER[0], S // 2, S, "y0b")
-        quantize_w1(nc.scalar.copy, 0, 2)
-        quantize_w1(nc.scalar.copy, 3, 4)
+        w1_mx = {**w1_mx, **quantize_weights(nc.scalar.copy, w1_raw, slice(0, 2), "w1_second")}
         project_text(ORDER[1], 0, S, "y1")
-
-        w2_bf = keep.tile([P, PACK * H], BF16, name="w2_bf", align_bytes=64)
-        w2_codes = keep.tile([P, H], I32, name="w2_codes", align_bytes=64)
-        w2_plane = keep.tile([P, H], U8, name="w2_plane", align_bytes=64)
-        cast_weights(nc.scalar.copy, w2_bf, w2_raw, 0, PACK)
-        quantize(nc, w2_codes[:], w2_plane[:], w2_bf[:])
+        w2_mx = quantize_weights(nc.scalar.copy, w2_raw, slice(0, PACK), "w2")
+        w1_mx = {**w1_mx, **quantize_weights(nc.scalar.copy, w1_raw, slice(3, 4), "y0a")}
 
         starts = [sum(CHUNKS[:c]) for c in range(len(CHUNKS))]
         z_bf = [keep.tile([P, n, PACK], BF16, name="z_bf%d" % c, align_bytes=64) for c, n in enumerate(CHUNKS)]
 
-        def regroup(copy, t, c):
-            copy(out=z_bf[c][:, :, t], in_=z[t][:, starts[c] : starts[c] + CHUNKS[c]])
+        def regroup(copy, t, c, part=slice(None)):
+            copy(out=z_bf[c][:, part, t], in_=z[t][:, starts[c] : starts[c] + CHUNKS[c]][:, part])
 
         project_text(ORDER[2], 0, S, "late")
         for t in ORDER[:3]:
@@ -148,7 +142,7 @@ def tile_picked_interl_relu_po_kernel(
         for c in range(len(CHUNKS)):
             regroup(nc.scalar.copy, ORDER[0], c)
         bank = proj.tile([P, S], F32, name="bank", tag="bank")
-        one_pass(nc, bank[:], w2_codes, w2_plane, ORDER[3], img_codes[:], img_scales[:])
+        one_pass(nc, bank[:], *w2_mx[ORDER[3]], img_codes[:], img_scales[:])
         for half, t in enumerate(ORDER[1:3]):
             for c in range(len(CHUNKS)):
                 regroup(nc.scalar.copy, t, c)
@@ -156,8 +150,8 @@ def tile_picked_interl_relu_po_kernel(
             eb = keep.tile([P, S // 2], F32, name="eb", tag="z%d" % (ORDER[0] if half == 0 else t), align_bytes=64)
             nc.scalar.activation(out=eb[:], in_=bank[:, j0:j1], func=RELU)
             nc.vector.tensor_copy(z[ORDER[3]][:].indirect(lb_sb[:, j0 // 16 : j1 // 16]), eb[:])
-        for c in SCALAR_CHUNKS:
-            regroup(nc.scalar.copy, ORDER[3], c)
+        regroup(nc.scalar.copy, ORDER[3], 2)
+        regroup(nc.scalar.copy, ORDER[3], 3)
 
         out_rows = out_0.rearrange("(p t) w -> p t w", t=PACK)
         out_words = out_1[0].rearrange("p n t -> p (n t)").bitcast(I32)

@@ -20,7 +20,8 @@ CHUNKS = (128, 256, 256, 256, 128)
 VECTOR_BANK = (1, 2)
 BANK_STORES = (1,)
 WORD_STORES = {2: 0, 3: 640, 4: 896}
-ORDER = (2, 0, 1, 3)
+ORDER = (0, 1, 2, 3)
+LAST_PIECE = 128
 
 
 def load_scale_rows(nc, plane, rows):
@@ -97,7 +98,7 @@ def tile_picked_interl_relu_po_kernel(
             quantize(nc, codes[:], plane[:], grouped[:])
             return {t: (codes, plane, i) for i, t in enumerate(range(PACK)[slots])}
 
-        w1_mx = quantize_weights(nc.vector.tensor_copy, w1_raw, slice(2, 3), "w1_first")
+        w1_mx = quantize_weights(nc.vector.tensor_copy, w1_raw, slice(0, 1), "w1_first")
 
         w3_codes = keep.tile([P, N], I32, name="w3_codes", align_bytes=64)
         w3_dealt = keep.tile([P, N], U8, name="w3_dealt", align_bytes=64)
@@ -124,7 +125,7 @@ def tile_picked_interl_relu_po_kernel(
 
         project_text(ORDER[0], 0, S // 2, "y0a")
         project_text(ORDER[0], S // 2, S, "y0b")
-        w1_mx = {**w1_mx, **quantize_weights(nc.scalar.copy, w1_raw, slice(0, 2), "w1_second")}
+        w1_mx = {**w1_mx, **quantize_weights(nc.scalar.copy, w1_raw, slice(1, 3), "w1_second")}
         project_text(ORDER[1], 0, S, "y1")
         w2_mx = quantize_weights(nc.scalar.copy, w2_raw, slice(0, PACK), "w2")
         w1_mx = {**w1_mx, **quantize_weights(nc.scalar.copy, w1_raw, slice(3, 4), "y0a")}
@@ -139,17 +140,22 @@ def tile_picked_interl_relu_po_kernel(
         for t in ORDER[:3]:
             project_image(t, "eb%d" % t)
         project_text(ORDER[3], 0, S, "y3")
-        for c in range(len(CHUNKS)):
-            regroup(nc.scalar.copy, ORDER[0], c)
         bank = proj.tile([P, S], F32, name="bank", tag="bank")
         one_pass(nc, bank[:], *w2_mx[ORDER[3]], img_codes[:], img_scales[:])
-        for half, t in enumerate(ORDER[1:3]):
-            for c in range(len(CHUNKS)):
-                regroup(nc.scalar.copy, t, c)
-            j0, j1 = half * S // 2, (half + 1) * S // 2
-            eb = keep.tile([P, S // 2], F32, name="eb", tag="z%d" % (ORDER[0] if half == 0 else t), align_bytes=64)
+
+        def place_image(j0, j1, tag):
+            eb = keep.tile([P, j1 - j0], F32, name="eb", tag=tag, align_bytes=64)
             nc.scalar.activation(out=eb[:], in_=bank[:, j0:j1], func=RELU)
             nc.vector.tensor_copy(z[ORDER[3]][:].indirect(lb_sb[:, j0 // 16 : j1 // 16]), eb[:])
+
+        place_image(0, S - LAST_PIECE, "eb3")
+        z_rows = keep.tile([P, PACK - 1, U], BF16, name="z_rows", tag="z_rows", align_bytes=64)
+        for t in range(PACK - 1):
+            nc.scalar.copy(out=z_rows[:, t, :], in_=z[t][:])
+        for c, n in enumerate(CHUNKS):
+            nc.scalar.copy(out=z_bf[c][:, :, 0 : PACK - 1].rearrange("p (c i) t -> p c t i", i=4),
+                           in_=z_rows[:, :, starts[c] : starts[c] + n].rearrange("p t (c i) -> p c t i", i=4))
+        place_image(S - LAST_PIECE, S, "z_rows")
         regroup(nc.scalar.copy, ORDER[3], 2)
         regroup(nc.scalar.copy, ORDER[3], 3)
 

@@ -24,11 +24,10 @@ ORDER = (0, 1, 2, 3)
 LAST_PIECE = 128
 
 
-def load_scale_rows(nc, plane, rows):
-    width = rows.shape[1] // 4
+def load_scale_rows(nc, memset, plane, rows):
+    memset(plane[:].bitcast(I32), 0)
     for q in range(4):
-        src = rows[4 * q : 4 * q + 4, :].bitcast(I32).unsqueeze(0).to_broadcast([8, 4, width])
-        nc.sync.dma_start(out=plane[32 * q : 32 * q + 32, :].bitcast(I32), in_=src)
+        nc.sync.dma_start(out=plane[32 * q : 32 * q + 4, :].bitcast(I32), in_=rows[4 * q : 4 * q + 4, :].bitcast(I32))
 
 
 def cast_weights(copy, grouped, raw, slots):
@@ -69,13 +68,13 @@ def tile_picked_interl_relu_po_kernel(
         w3_table = keep.tile([P, N], I32, name="w3_table", align_bytes=64)
         w3_plane = keep.tile([P, N], U8, name="w3_plane", align_bytes=64)
 
-        load_scale_rows(nc, x_plane, x_scales[0])
         nc.sync.dma_start(offs_sb[:], offs)
         nc.sync.dma_start(img_sb[:], img)
+        load_scale_rows(nc, nc.gpsimd.memset, x_plane, x_scales[0])
         nc.sync.dma_start(out=x_table[:], in_=x_words[0].rearrange("p n t -> p (n t)").bitcast(I32))
         nc.sync.dma_start(out=w1_raw[:], in_=w1.rearrange("(p j) c -> p j c", j=PACK))
         nc.sync.dma_start(out=w3_table[:], in_=w3_words[0].rearrange("p n t -> p (n t)").bitcast(I32))
-        load_scale_rows(nc, w3_plane, w3_scales[0])
+        load_scale_rows(nc, nc.vector.memset, w3_plane, w3_scales[0])
         nc.sync.dma_start(la_sb[:], la)
         nc.sync.dma_start(lb_sb[:], lb)
         nc.sync.dma_start(out=w2_raw[:], in_=w2.rearrange("(p j) c -> p j c", j=PACK))

from contextlib import ExitStack

import concourse.mybir as mybir

K, T, S, N, H, U = 512, 2048, 512, 512, 512, 1024
FLOPS = 2 * K * H * S * 2 + 2 * H * N * U

F32 = mybir.dt.float32
BF16 = mybir.dt.bfloat16
I32 = mybir.dt.int32
U32 = mybir.dt.uint32
U16 = mybir.dt.uint16
U8 = mybir.dt.uint8
FP8X4 = mybir.dt.float8_e4m3fn_x4
RELU = mybir.ActivationFunctionType.Relu

P = 128
PACK = 4
CHUNKS = (128, 256, 256, 256, 128)
VECTOR_BANK = (1, 2)
BANK_STORES = (1,)
WORD_STORES = {2: 0, 3: 640, 4: 896}
ORDER = (0, 1, 2, 3)
LAST_PIECE = 128


def load_scale_rows(nc, memset, plane, rows):
    memset(plane[:].bitcast(I32), 0)
    for q in range(4):
        nc.sync.dma_start(out=plane[32 * q : 32 * q + 4, :].bitcast(I32), in_=rows[4 * q : 4 * q + 4, :].bitcast(I32))


def cast_weights(copy, grouped, raw, slots):
    copy(
        out=grouped[:].rearrange("p (t m j) -> p m t j", m=P, j=PACK),
        in_=raw[:].rearrange("p j (m t) -> p m t j", t=PACK)[:, :, slots],
    )


def quantize(nc, codes, scales, values):
    nc.vector.quantize_mx(out=codes.bitcast(FP8X4), scales=scales, in_=values)


def one_pass(nc, out, w_codes, w_scales, t, codes, scales):
    cols = slice(P * t, P * (t + 1))
    nc.tensor.matmul_mx(out=out, lhsT=w_codes[:, cols].bitcast(FP8X4), lhsT_scale=w_scales[:, cols],
                        rhs=codes.bitcast(FP8X4), rhs_scale=scales, start=True, stop=True)


def tile_picked_interl_relu_po_kernel(
    tc, x_words, x_scales, w1, w2, w3_words, w3_scales, offs, img, la, lb, out_0, out_1, out_2
):
    nc = tc.nc
    with ExitStack() as ctx:
        lists = ctx.enter_context(tc.tile_pool(name="lists", bufs=1))
        keep = ctx.enter_context(tc.tile_pool(name="keep", bufs=1))
        proj = ctx.enter_context(tc.psum_pool(name="proj", bufs=3))
        last = ctx.enter_context(tc.psum_pool(name="last", bufs=5))

        offs_sb = lists.tile([P, S // 16], U16, name="offs_sb")
        img_sb = lists.tile([P, S // 16], U16, name="img_sb")
        la_sb = lists.tile([P, S // 16], U16, name="la_sb")
        lb_sb = lists.tile([P, S // 16], U16, name="lb_sb")
        x_plane = keep.tile([P, T], U8, name="x_plane", align_bytes=64)
        x_table = keep.tile([P, T], I32, name="x_table", align_bytes=64)
        w1_raw = keep.tile([P, PACK, H], F32, name="w1_raw", align_bytes=64)
        w2_raw = keep.tile([P, PACK, H], F32, name="w2_raw", tag="late", align_bytes=64)
        w3_table = keep.tile([P, N], I32, name="w3_table", align_bytes=64)
        w3_plane = keep.tile([P, N], U8, name="w3_plane", align_bytes=64)

        nc.sync.dma_start(offs_sb[:], offs)
        nc.sync.dma_start(img_sb[:], img)
        load_scale_rows(nc, nc.gpsimd.memset, x_plane, x_scales[0])
        nc.sync.dma_start(out=x_table[:], in_=x_words[0].rearrange("p n t -> p (n t)").bitcast(I32))
        nc.sync.dma_start(out=w1_raw[:], in_=w1.rearrange("(p j) c -> p j c", j=PACK))
        nc.sync.dma_start(out=w3_table[:], in_=w3_words[0].rearrange("p n t -> p (n t)").bitcast(I32))
        load_scale_rows(nc, nc.vector.memset, w3_plane, w3_scales[0])
        nc.sync.dma_start(la_sb[:], la)
        nc.sync.dma_start(lb_sb[:], lb)
        nc.sync.dma_start(out=w2_raw[:], in_=w2.rearrange("(p j) c -> p j c", j=PACK))

        txt_scales = keep.tile([P, S], U8, name="txt_scales", align_bytes=64)
        img_scales = keep.tile([P, S], U8, name="img_scales", align_bytes=64)
        txt_codes = keep.tile([P, S], I32, name="txt_codes", align_bytes=64)
        img_codes = keep.tile([P, S], I32, name="img_codes", align_bytes=64)
        nc.vector.tensor_copy(txt_scales[:], x_plane[:].indirect(offs_sb[:]))
        nc.vector.tensor_copy(img_scales[:], x_plane[:].indirect(img_sb[:]))
        nc.vector.tensor_copy(txt_codes[:].bitcast(U32), x_table[:].bitcast(U32).indirect(offs_sb[:]))
        nc.vector.tensor_copy(img_codes[:].bitcast(U32), x_table[:].bitcast(U32).indirect(img_sb[:]))

        def quantize_weights(copy, raw, slots, tag):
            count = len(range(PACK)[slots])
            grouped = keep.tile([P, count * H], BF16, name="grouped", tag=tag, align_bytes=64)
            codes = keep.tile([P, count * P], I32, name="codes", tag=tag + "_codes", align_bytes=64)
            plane = keep.tile([P, count * P], U8, name="plane", tag=tag + "_plane", align_bytes=64)
            cast_weights(copy, grouped, raw, slots)
            quantize(nc, codes[:], plane[:], grouped[:])
            return {t: (codes, plane, i) for i, t in enumerate(range(PACK)[slots])}

        w1_mx = quantize_weights(nc.vector.tensor_copy, w1_raw, slice(0, 1), "w1_first")

        w3_codes = keep.tile([P, N], I32, name="w3_codes", align_bytes=64)
        w3_dealt = keep.tile([P, N], U8, name="w3_dealt", align_bytes=64)
        nc.vector.tensor_copy(out=w3_codes[:].rearrange("p (t m) -> p m t", t=PACK),
                              in_=w3_table[:].rearrange("p (m t) -> p m t", t=PACK))
        nc.vector.tensor_copy(out=w3_dealt[:].rearrange("p (t m) -> p t m", t=PACK),
                              in_=w3_plane[:].rearrange("p (m t) -> p t m", t=PACK))

        z = [keep.tile([P, U], F32, name="z%d" % t, align_bytes=64) for t in range(PACK)]

        def project_text(t, j0, j1, tag):
            bank = proj.tile([P, j1 - j0], F32, name="bank", tag="bank")
            one_pass(nc, bank[:], *w1_mx[t], txt_codes[:, j0:j1], txt_scales[:, j0:j1])
            y = keep.tile([P, j1 - j0], F32, name="y", tag=tag, align_bytes=64)
            nc.scalar.copy(out=y[:], in_=bank[:])
            nc.vector.tensor_copy(z[t][:].indirect(la_sb[:, j0 // 16 : j1 // 16]), y[:])

        def project_image(t, tag):
            bank = proj.tile([P, S], F32, name="bank", tag="bank")
            one_pass(nc, bank[:], *w2_mx[t], img_codes[:], img_scales[:])
            eb = keep.tile([P, S], F32, name="eb", tag=tag, align_bytes=64)
            nc.scalar.activation(out=eb[:], in_=bank[:], func=RELU)
            nc.vector.tensor_copy(z[t][:].indirect(lb_sb[:]), eb[:])

        project_text(ORDER[0], 0, S // 2, "y0a")
        project_text(ORDER[0], S // 2, S, "y0b")
        w1_mx = {**w1_mx, **quantize_weights(nc.scalar.copy, w1_raw, slice(1, 3), "w1_second")}
        project_text(ORDER[1], 0, S, "y1")
        w2_mx = quantize_weights(nc.scalar.copy, w2_raw, slice(0, PACK), "w2")
        w1_mx = {**w1_mx, **quantize_weights(nc.scalar.copy, w1_raw, slice(3, 4), "y0a")}

        starts = [sum(CHUNKS[:c]) for c in range(len(CHUNKS))]
        z_bf = [keep.tile([P, n, PACK], BF16, name="z_bf%d" % c, align_bytes=64) for c, n in enumerate(CHUNKS)]

        def regroup(copy, t, c, part=slice(None)):
            copy(out=z_bf[c][:, part, t], in_=z[t][:, starts[c] : starts[c] + CHUNKS[c]][:, part])

        project_text(ORDER[2], 0, S, "late")
        for t in ORDER[:3]:
            project_image(t, "eb%d" % t)
        project_text(ORDER[3], 0, S, "y3")
        bank = proj.tile([P, S], F32, name="bank", tag="bank")
        one_pass(nc, bank[:], *w2_mx[ORDER[3]], img_codes[:], img_scales[:])

        def place_image(j0, j1, tag):
            eb = keep.tile([P, j1 - j0], F32, name="eb", tag=tag, align_bytes=64)
            nc.scalar.activation(out=eb[:], in_=bank[:, j0:j1], func=RELU)
            nc.vector.tensor_copy(z[ORDER[3]][:].indirect(lb_sb[:, j0 // 16 : j1 // 16]), eb[:])

        place_image(0, S - LAST_PIECE, "eb3")
        z_rows = keep.tile([P, PACK - 1, U], BF16, name="z_rows", tag="z_rows", align_bytes=64)
        for t in range(PACK - 1):
            nc.scalar.copy(out=z_rows[:, t, :], in_=z[t][:])
        for c, n in enumerate(CHUNKS):
            nc.scalar.copy(out=z_bf[c][:, :, 0 : PACK - 1].rearrange("p (c i) t -> p c t i", i=4),
                           in_=z_rows[:, :, starts[c] : starts[c] + n].rearrange("p t (c i) -> p c t i", i=4))
        place_image(S - LAST_PIECE, S, "z_rows")
        regroup(nc.scalar.copy, ORDER[3], 2)
        regroup(nc.scalar.copy, ORDER[3], 3)

        out_rows = out_0.rearrange("(p t) w -> p t w", t=PACK)
        out_words = out_1[0].rearrange("p n t -> p (n t)").bitcast(I32)
        out_codes = keep.tile([P, U], I32, name="out_codes", align_bytes=64)
        out_plane = keep.tile([P, U], U8, name="out_plane", align_bytes=64)

        def quantize_z(c):
            n = CHUNKS[c]
            z_codes = keep.tile([P, n], I32, name="z_codes%d" % c, align_bytes=64)
            z_plane = keep.tile([P, n], U8, name="z_plane%d" % c, align_bytes=64)
            quantize(nc, z_codes[:], z_plane[:], z_bf[c][:].rearrange("p n t -> p (n t)"))
            return z_codes, z_plane

        def multiply(c, z_codes, z_plane):
            n = CHUNKS[c]
            cols = slice(starts[c], starts[c] + n)
            result = keep.tile([P, PACK, n], F32, name="result%d" % c, align_bytes=64)
            rounded = keep.tile([P, n, PACK], BF16, name="rounded%d" % c, align_bytes=64)
            per_bank = 512 // n
            for t0 in range(0, PACK, per_bank):
                if c < 2:
                    acc = proj.tile([P, per_bank, n], F32, name="acc", tag="bank")
                else:
                    acc = last.tile([P, per_bank, n], F32, name="acc", tag="acc")
                for i in range(per_bank):
                    one_pass(nc, acc[:, i, :], w3_codes, w3_dealt, t0 + i, z_codes[:], z_plane[:])
                if c == len(CHUNKS) - 1:
                    nc.scalar.copy(out=rounded[:], in_=acc[:].rearrange("p t n -> p n t"))
                copy = nc.vector.tensor_copy if (c, t0) == VECTOR_BANK else nc.scalar.copy
                copy(out=result[:, t0 : t0 + per_bank, :], in_=acc[:])
                if c in BANK_STORES:
                    nc.sync.dma_start(out=out_rows[:, t0 : t0 + per_bank, cols], in_=result[:, t0 : t0 + per_bank, :])
            if c not in BANK_STORES:
                nc.sync.dma_start(out=out_rows[:, :, cols], in_=result[:])
            if c < len(CHUNKS) - 1:
                nc.vector.tensor_copy(out=rounded[:].rearrange("p (c i) t -> p c t i", i=4),
                                      in_=result[:].rearrange("p t (c i) -> p c t i", i=4))
            quantize(nc, out_codes[:, cols], out_plane[:, cols], rounded[:].rearrange("p n t -> p (n t)"))
            if c in WORD_STORES:
                done = slice(WORD_STORES[c], starts[c] + n)
                nc.sync.dma_start(out=out_words[:, done], in_=out_codes[:, done])

        regroup(nc.vector.tensor_copy, ORDER[3], 0)
        regroup(nc.vector.tensor_copy, ORDER[3], 1)
        z_quantised = [quantize_z(c) for c in range(3)]
        regroup(nc.vector.tensor_copy, ORDER[3], 4)
        z_quantised.extend(quantize_z(c) for c in range(3, 5))
        for c in range(len(CHUNKS)):
            multiply(c, *z_quantised[c])
        for q in range(4):
            queue = nc.scalar if q % 2 else nc.sync
            queue.dma_start(out=out_2[0, 4 * q : 4 * q + 4, :].bitcast(I32),
                            in_=out_plane[32 * q : 32 * q + 4, :].bitcast(I32))
